import numpy as np
import ml_dtypes


def mxq(x, axis, fmt="e4m3"):
    dtype, down = {"e4m3": (ml_dtypes.float8_e4m3fn, 7), "e5m2": (ml_dtypes.float8_e5m2, 14)}[fmt]
    v = np.moveaxis(np.asarray(x, np.float32).astype(ml_dtypes.bfloat16).astype(np.float64), axis, -1)
    blocks = v.reshape(v.shape[:-1] + (-1, 32))
    amax = np.abs(blocks).max(-1, keepdims=True)
    byte = np.maximum(np.where(amax > 0, np.frexp(amax)[1] - 1 + 127, 0) - down, 1)
    scale = np.exp2(byte - 127.0)
    codes = (blocks / scale).astype(np.float32).astype(dtype).astype(np.float64)
    return np.moveaxis((codes * scale).reshape(v.shape), -1, axis)


WIDE = False


def mx_kscale(k):
    if not WIDE:
        return np.ones(k)
    levels = np.array([10, -10, 5, -5, 0])
    if k % 512:
        return np.exp2(np.random.permutation(np.resize(levels, k // 32))).repeat(32)
    a = np.empty((k // 512, 16))
    for p in range(k // 512):
        a[p, :8] = np.random.permutation(np.resize(levels, 8))
        for g in range(8):
            far = levels[np.abs(levels - a[p, g]) >= 10]
            a[p, g + 8] = far[np.random.randint(len(far))]
    return np.exp2(a.ravel()).repeat(32)


def f64(x):
    return np.asarray(x).astype(np.float64)


def striped(idx):
    return np.tile(idx.reshape(-1, 16).T, (8, 1)).astype(np.uint16)


def unstriped(offs):
    return offs[:16].T.reshape(-1).astype(np.int64)


def d_silu(v):
    s = 1.0 / (1.0 + np.exp(-np.maximum(v, -700.0)))
    return s * (1.0 + v * (1.0 - s))


K, T, E, C, H, N = 512, 640, 2, 256, 1024, 1536


def by_expert(wq, xq):
    return np.concatenate([wq[e].T @ xq[:, e * C:(e + 1) * C] for e in range(E)], axis=1)


def setup_inputs():
    n = np.random.standard_normal
    s = mx_kscale(N)[:, None]
    u = mx_kscale(H)
    return {
        "dyT": (n((N, T)) * s).astype(np.float32),
        "a": n((H, E * C)).astype(np.float32),
        "w2": (n((E, N, H)) / np.sqrt(N) / s[None] * u[None, None, :]).astype(np.float32),
        "w1": (n((E, H, K)) / np.sqrt(H) / u[None, :, None]).astype(np.float32),
        "gate": np.tile(np.random.uniform(0.2, 1.0, E * C), (N, 1)).astype(np.float32),
        "offs": striped(np.random.permutation(T)[:E * C]),
    }


def reference(dyT, a, w2, w1, gate, offs):
    idx = unstriped(offs)
    gq = mxq(f64(gate) * f64(dyT)[:, idx], 0, "e4m3")
    dh = by_expert(mxq(f64(w2), 1, "e4m3"), gq)
    da = dh * d_silu(f64(a))
    dx = by_expert(mxq(f64(w1), 1, "e4m3"), mxq(da, 0, "e4m3"))
    out = np.zeros((K, T))
    out[:, idx] = dx
    return out

@@ -1,0 +1,268 @@
+from contextlib import ExitStack
+
+import concourse.mybir as mybir
+
+N, T, H, K, E, C = 1536, 640, 1024, 512, 2, 256
+SLOTS = E * C
+FLOPS = 2 * SLOTS * (N * H + H * K)
+BYTES = 4 * (N * T + H * SLOTS + E * N * H + E * H * K + SLOTS + K * T) + 2 * 128 * (SLOTS // 16)
+
+F32 = mybir.dt.float32
+BF16 = mybir.dt.bfloat16
+U32 = mybir.dt.uint32
+U16 = mybir.dt.uint16
+U8 = mybir.dt.uint8
+FP8X4 = mybir.dt.float8_e4m3fn_x4
+MULT = mybir.AluOpType.mult
+SUB = mybir.AluOpType.subtract
+SIGMOID = mybir.ActivationFunctionType.Sigmoid
+SILU = mybir.ActivationFunctionType.Silu
+
+W2_ENGINE = "SVSVSVSVSSSS"
+W1_ENGINE = "SSSSSSSS"
+P = 128
+J = 4
+PASS = P * J
+G = N // PASS
+HP = H // PASS
+KT = K // P
+KH = K // 2
+
+
+def tile_moe_bdx_mlp_silu_kernel(tc, dyT, a, w2, w1, gate, offs, out):
+    nc = tc.nc
+    with ExitStack() as ctx:
+        held = ctx.enter_context(tc.tile_pool(name="held", bufs=1))
+        codes = ctx.enter_context(tc.tile_pool(name="codes", bufs=4))
+        ring = ctx.enter_context(tc.tile_pool(name="ring", bufs=3))
+        stage = ctx.enter_context(tc.tile_pool(name="stage", bufs=2))
+        psum = ctx.enter_context(tc.psum_pool(name="psum", bufs=4))
+
+        offsets = held.tile([P, SLOTS // 16], U16, name="offsets")
+        nc.sync.dma_start(offsets[:], offs)
+        gates = held.tile([P, SLOTS], F32, name="gates")
+        nc.sync.dma_start(gates[:], gate[0:P, :])
+
+        one = held.tile([P, 1], F32, name="one")
+        nc.vector.memset(one[:], 0.0)
+        warm = held.tile([P, 1], F32, name="warm")
+        nc.scalar.activation(warm[:], one[:], SIGMOID)
+
+        outs = []
+        for kt in range(KT):
+            o = held.tile([P, T], F32, name=f"out{kt}")
+            nc.gpsimd.memset(o[:], 0.0)
+            outs.append(o)
+
+        def quant(out_c, out_s, src):
+            nc.vector.quantize_mx(out=out_c.bitcast(FP8X4), scales=out_s, in_=src)
+
+        dy, gg, gq, w2raw, w2q, w1raw, w1q, dq = {}, {}, {}, {}, {}, {}, {}, {}
+
+        def load_dy(g, j):
+            dy[g, j] = ring.tile([P, T], F32, name="dy", bufs=8)
+            nc.sync.dma_start(dy[g, j][:], dyT[g * PASS : (g + 1) * PASS, :].rearrange("(p j) t -> p j t", j=J)[:, j, :])
+
+        act = held.tile([P, HP, J, SLOTS], F32, name="act")
+        sig = held.tile([P, HP, J, SLOTS], F32, name="sig")
+        PAIRS = [slice(0, 2), slice(2, 4)]
+
+        def load_a(h):
+            rows = a[h * PASS : (h + 1) * PASS, :].rearrange("(p t) n -> p t n", t=J)
+            for pair in PAIRS:
+                nc.sync.dma_start(act[:, h, pair, :], rows[:, pair, :])
+
+        def load_w2(e, g):
+            w2raw[e, g] = ring.tile([P, J, H], F32, name="w2raw", bufs=3)
+            nc.sync.dma_start(w2raw[e, g][:], w2[e, g * PASS : (g + 1) * PASS, :].rearrange("(p j) i -> p j i", j=J))
+
+        def load_w1(e, kh):
+            w1raw[e, kh] = ring.tile([P, HP, J, KH], F32, name="w1raw", bufs=3)
+            rows = w1[e, :, kh * KH : (kh + 1) * KH].rearrange("(h p j) k -> p h j k", p=P, j=J)
+            for h in range(HP):
+                nc.sync.dma_start(w1raw[e, kh][:, h], rows[:, h])
+
+        def lay(engine, out_, in_):
+            if engine == "V":
+                nc.vector.tensor_copy(out_, in_)
+            else:
+                nc.scalar.copy(out_, in_)
+
+        def gather(g, j):
+            if (g) not in gg:
+                gg[g] = stage.tile([P, J, SLOTS], F32, name="gg", bufs=2)
+            nc.vector.tensor_tensor(gg[g][:, j, :], dy[g, j][:].indirect(offsets[:]), gates[:], MULT)
+
+        def g_codes(g):
+            gb = stage.tile([P, SLOTS * J], BF16, name="gb", bufs=2, align_bytes=64)
+            nc.scalar.copy(
+                out=gb[:].rearrange("p (c i j) -> p c j i", i=4, j=J),
+                in_=gg[g][:].rearrange("p j (c i) -> p c j i", i=4),
+            )
+            gc = held.tile([P, SLOTS], U32, name=f"gc{g}", align_bytes=64)
+            gs = held.tile([P, SLOTS], U8, name=f"gs{g}", align_bytes=64)
+            quant(gc[:], gs[:], gb[:])
+            gq[g] = gc, gs
+
+        def sigmoids(h):
+            for pair in PAIRS:
+                nc.scalar.activation(sig[:, h, pair, :], act[:, h, pair, :], SIGMOID)
+
+        def silus(i):
+            nc.scalar.activation(act[:, :, PAIRS[i], :], act[:, :, PAIRS[i], :], SILU, scale=-1.0)
+
+        def derivative(h):
+            nc.vector.scalar_tensor_tensor(sig[:, h], act[:, h], 1.0, sig[:, h], SUB, MULT)
+
+        def w2_codes(e, g, h):
+            if (e, g) not in w2q:
+                wc = codes.tile([P, H], U32, name="w2c", bufs=4, align_bytes=64)
+                ws = codes.tile([P, H], U8, name="w2s", bufs=4, align_bytes=64)
+                w2q[e, g] = wc, ws
+            wc, ws = w2q[e, g]
+            cols = slice(h * PASS, (h + 1) * PASS)
+            wb = stage.tile([P, PASS * J], BF16, name="wb", bufs=5, align_bytes=64)
+            lay(
+                W2_ENGINE[(e * G + g) * HP + h],
+                wb[:].rearrange("p (t m j) -> p m j t", t=4, j=J),
+                w2raw[e, g][:, :, cols].rearrange("p j (m t) -> p m j t", t=4),
+            )
+            quant(wc[:, cols], ws[:, cols], wb[:])
+
+        def w1_codes(e, kh):
+            wc = codes.tile([P, HP * KH], U32, name="w1c", bufs=4, align_bytes=64)
+            ws = codes.tile([P, HP * KH], U8, name="w1s", bufs=4, align_bytes=64)
+            wb = stage.tile([P, PASS * J], BF16, name="wb", bufs=5, align_bytes=64)
+            for h in range(HP):
+                lay(
+                    W1_ENGINE[(e * 2 + kh) * HP + h],
+                    wb[:, h * KH * J : (h + 1) * KH * J].rearrange("p (c i j) -> p c j i", i=4, j=J),
+                    w1raw[e, kh][:, h].rearrange("p j (c i) -> p c j i", i=4),
+                )
+            quant(wc[:], ws[:], wb[:])
+            w1q[e, kh] = wc, ws
+
+        def first_product(e, h):
+            db = stage.tile([P, C * J], BF16, name="db", bufs=2, align_bytes=64)
+            for half in range(2):
+                n0 = e * C + half * P
+                bank = psum.tile([P, J, P], F32, name="dh", bufs=4)
+                for t in range(J):
+                    m = slice(h * PASS + t * P, h * PASS + (t + 1) * P)
+                    for g in range(G):
+                        wc, ws = w2q[e, g]
+                        gc, gs = gq[g]
+                        nc.tensor.matmul_mx(
+                            out=bank[:, t, :],
+                            lhsT=wc[:, m].bitcast(FP8X4),
+                            lhsT_scale=ws[:, m],
+                            rhs=gc[:, n0 : n0 + P].bitcast(FP8X4),
+                            rhs_scale=gs[:, n0 : n0 + P],
+                            start=(g == 0),
+                            stop=(g == G - 1),
+                        )
+                nc.vector.scalar_tensor_tensor(
+                    db[:, half * PASS : (half + 1) * PASS].rearrange("p (n t) -> p n t", t=J),
+                    bank[:].rearrange("p t n -> p n t"),
+                    -1.0,
+                    sig[:, h, :, n0 : n0 + P].rearrange("p t n -> p n t"),
+                    MULT,
+                    MULT,
+                )
+            dc = codes.tile([P, C], U32, name="dc", bufs=4, align_bytes=64)
+            ds = codes.tile([P, C], U8, name="ds", bufs=4, align_bytes=64)
+            quant(dc[:], ds[:], db[:])
+            dq[e, h] = dc, ds
+
+        def second_product(e, kh):
+            wc, ws = w1q[e, kh]
+            for q in range(2):
+                acc = psum.tile([P, C], F32, name="dx", bufs=4)
+                for h in range(HP):
+                    m = slice(h * KH + q * P, h * KH + (q + 1) * P)
+                    dc, ds = dq[e, h]
+                    nc.tensor.matmul_mx(
+                        out=acc[:],
+                        lhsT=wc[:, m].bitcast(FP8X4),
+                        lhsT_scale=ws[:, m],
+                        rhs=dc[:].bitcast(FP8X4),
+                        rhs_scale=ds[:],
+                        start=(h == 0),
+                        stop=(h == HP - 1),
+                    )
+                dx = stage.tile([P, C], F32, name="dxs", bufs=4)
+                nc.scalar.copy(out=dx[:], in_=acc[:])
+                kt = 2 * kh + q
+                nc.vector.tensor_copy(outs[kt][:].indirect(offsets[:, e * (C // 16) : (e + 1) * (C // 16)]), dx[:])
+                if e == E - 1:
+                    nc.sync.dma_start(out[kt * P : (kt + 1) * P, :], outs[kt][:])
+
+        load_dy(0, 0)
+        load_dy(0, 1)
+        load_dy(0, 2)
+        load_dy(0, 3)
+        load_a(0)
+        load_dy(1, 0)
+        load_dy(1, 1)
+        load_dy(1, 2)
+        load_dy(1, 3)
+        gather(0, 0)
+        gather(0, 1)
+        gather(0, 2)
+        gather(0, 3)
+        g_codes(0)
+        sigmoids(0)
+        load_a(1)
+        load_dy(2, 0)
+        load_dy(2, 1)
+        load_dy(2, 2)
+        load_dy(2, 3)
+        gather(1, 0)
+        gather(1, 1)
+        gather(1, 2)
+        gather(1, 3)
+        sigmoids(1)
+        load_w2(0, 0)
+        load_w2(0, 1)
+        gather(2, 0)
+        gather(2, 1)
+        gather(2, 2)
+        gather(2, 3)
+        g_codes(1)
+        silus(0)
+        silus(1)
+        load_w2(0, 2)
+        g_codes(2)
+        w2_codes(0, 0, 0)
+        w2_codes(0, 0, 1)
+        derivative(0)
+        derivative(1)
+        w2_codes(0, 1, 0)
+        w2_codes(0, 1, 1)
+        load_w1(0, 0)
+        load_w1(0, 1)
+        w2_codes(0, 2, 0)
+        w2_codes(0, 2, 1)
+        load_w2(1, 0)
+        w1_codes(0, 0)
+        w1_codes(0, 1)
+        first_product(0, 0)
+        first_product(0, 1)
+        load_w2(1, 1)
+        w2_codes(1, 0, 0)
+        w2_codes(1, 0, 1)
+        second_product(0, 0)
+        load_w2(1, 2)
+        w2_codes(1, 1, 0)
+        w2_codes(1, 1, 1)
+        second_product(0, 1)
+        load_w1(1, 0)
+        load_w1(1, 1)
+        w2_codes(1, 2, 0)
+        w2_codes(1, 2, 1)
+        first_product(1, 0)
+        first_product(1, 1)
+        w1_codes(1, 0)
+        second_product(1, 0)
+        w1_codes(1, 1)
+        second_product(1, 1)

@@ -18,8 +18,8 @@ SUB = mybir.AluOpType.subtract
 SIGMOID = mybir.ActivationFunctionType.Sigmoid
 SILU = mybir.ActivationFunctionType.Silu
 
-W2_ENGINE = "SVSVSVSVSSSS"
-W1_ENGINE = "SSSSSSSS"
+W2_ENGINE = "SSVVVSSSSVSV"
+W1_ENGINE = "SVSVSSSS"
 P = 128
 J = 4
 PASS = P * J
@@ -197,72 +197,72 @@ def tile_moe_bdx_mlp_silu_kernel(tc, dyT, a, w2, w1, gate, offs, out):
                 if e == E - 1:
                     nc.sync.dma_start(out[kt * P : (kt + 1) * P, :], outs[kt][:])
 
-        load_dy(0, 0)
-        load_dy(0, 1)
-        load_dy(0, 2)
         load_dy(0, 3)
-        load_a(0)
-        load_dy(1, 0)
-        load_dy(1, 1)
+        load_dy(0, 2)
         load_dy(1, 2)
-        load_dy(1, 3)
-        gather(0, 0)
-        gather(0, 1)
-        gather(0, 2)
-        gather(0, 3)
-        g_codes(0)
-        sigmoids(0)
-        load_a(1)
-        load_dy(2, 0)
-        load_dy(2, 1)
-        load_dy(2, 2)
-        load_dy(2, 3)
+        load_dy(1, 0)
         gather(1, 0)
-        gather(1, 1)
-        gather(1, 2)
+        load_dy(1, 3)
+        load_a(0)
+        load_dy(1, 1)
+        load_dy(0, 0)
         gather(1, 3)
-        sigmoids(1)
-        load_w2(0, 0)
+        load_dy(0, 1)
+        gather(1, 2)
+        gather(1, 1)
+        gather(0, 2)
+        load_a(1)
+        gather(0, 3)
         load_w2(0, 1)
-        gather(2, 0)
-        gather(2, 1)
-        gather(2, 2)
-        gather(2, 3)
         g_codes(1)
-        silus(0)
+        load_dy(2, 3)
+        load_dy(2, 0)
+        gather(0, 0)
+        sigmoids(1)
+        gather(0, 1)
+        w2_codes(0, 1, 1)
+        load_dy(2, 2)
+        load_w2(0, 0)
+        load_dy(2, 1)
+        gather(2, 1)
+        sigmoids(0)
         silus(1)
         load_w2(0, 2)
-        g_codes(2)
+        silus(0)
         w2_codes(0, 0, 0)
         w2_codes(0, 0, 1)
-        derivative(0)
-        derivative(1)
-        w2_codes(0, 1, 0)
-        w2_codes(0, 1, 1)
-        load_w1(0, 0)
-        load_w1(0, 1)
         w2_codes(0, 2, 0)
-        w2_codes(0, 2, 1)
+        load_w1(0, 0)
+        gather(2, 3)
+        w2_codes(0, 1, 0)
+        gather(2, 2)
+        g_codes(0)
+        gather(2, 0)
+        g_codes(2)
+        derivative(0)
         load_w2(1, 0)
-        w1_codes(0, 0)
-        w1_codes(0, 1)
+        derivative(1)
+        w2_codes(0, 2, 1)
         first_product(0, 0)
-        first_product(0, 1)
-        load_w2(1, 1)
-        w2_codes(1, 0, 0)
+        w1_codes(0, 0)
         w2_codes(1, 0, 1)
-        second_product(0, 0)
-        load_w2(1, 2)
-        w2_codes(1, 1, 0)
+        load_w2(1, 1)
+        first_product(0, 1)
         w2_codes(1, 1, 1)
-        second_product(0, 1)
+        load_w2(1, 2)
+        load_w1(0, 1)
+        w2_codes(1, 0, 0)
         load_w1(1, 0)
-        load_w1(1, 1)
-        w2_codes(1, 2, 0)
+        w2_codes(1, 1, 0)
         w2_codes(1, 2, 1)
-        first_product(1, 0)
+        load_w1(1, 1)
+        second_product(0, 0)
+        w1_codes(0, 1)
         first_product(1, 1)
+        w2_codes(1, 2, 0)
         w1_codes(1, 0)
-        second_product(1, 0)
+        first_product(1, 0)
         w1_codes(1, 1)
+        second_product(0, 1)
         second_product(1, 1)
+        second_product(1, 0)

@@ -14,12 +14,14 @@ U16 = mybir.dt.uint16
 U8 = mybir.dt.uint8
 FP8X4 = mybir.dt.float8_e4m3fn_x4
 MULT = mybir.AluOpType.mult
+ADD = mybir.AluOpType.add
 SUB = mybir.AluOpType.subtract
 SIGMOID = mybir.ActivationFunctionType.Sigmoid
 SILU = mybir.ActivationFunctionType.Silu
 
-W2_ENGINE = "SSVVVSSSSVSV"
-W1_ENGINE = "SVSVSSSS"
+W2_ENGINE = "SSSSSSSSSSSS"
+W1_ENGINE = "SSSVSSVV"
+G_ENGINE = "VVV"
 P = 128
 J = 4
 PASS = P * J
@@ -85,6 +87,8 @@ def tile_moe_bdx_mlp_silu_kernel(tc, dyT, a, w2, w1, gate, offs, out):
         def lay(engine, out_, in_):
             if engine == "V":
                 nc.vector.tensor_copy(out_, in_)
+            elif engine == "G":
+                nc.gpsimd.tensor_scalar(out_, in_, 1.0, 0.0, MULT, ADD)
             else:
                 nc.scalar.copy(out_, in_)
 
@@ -95,9 +99,10 @@ def tile_moe_bdx_mlp_silu_kernel(tc, dyT, a, w2, w1, gate, offs, out):
 
         def g_codes(g):
             gb = stage.tile([P, SLOTS * J], BF16, name="gb", bufs=2, align_bytes=64)
-            nc.scalar.copy(
-                out=gb[:].rearrange("p (c i j) -> p c j i", i=4, j=J),
-                in_=gg[g][:].rearrange("p j (c i) -> p c j i", i=4),
+            lay(
+                G_ENGINE[g],
+                gb[:].rearrange("p (c i j) -> p c j i", i=4, j=J),
+                gg[g][:].rearrange("p j (c i) -> p c j i", i=4),
             )
             gc = held.tile([P, SLOTS], U32, name=f"gc{g}", align_bytes=64)
             gs = held.tile([P, SLOTS], U8, name=f"gs{g}", align_bytes=64)
@@ -108,11 +113,15 @@ def tile_moe_bdx_mlp_silu_kernel(tc, dyT, a, w2, w1, gate, offs, out):
             for pair in PAIRS:
                 nc.scalar.activation(sig[:, h, pair, :], act[:, h, pair, :], SIGMOID)
 
-        def silus(i):
-            nc.scalar.activation(act[:, :, PAIRS[i], :], act[:, :, PAIRS[i], :], SILU, scale=-1.0)
+        def silus(e):
+            part = act[:, :, :, e * C : (e + 1) * C].rearrange("p h t n -> p (h t) n")
+            nc.scalar.activation(part, part, SILU, scale=-1.0)
 
-        def derivative(h):
-            nc.vector.scalar_tensor_tensor(sig[:, h], act[:, h], 1.0, sig[:, h], SUB, MULT)
+        def derivative(e):
+            part = slice(e * C, (e + 1) * C)
+            x = act[:, :, :, part].rearrange("p h t n -> p (h t) n")
+            s = sig[:, :, :, part].rearrange("p h t n -> p (h t) n")
+            nc.vector.scalar_tensor_tensor(s, x, 1.0, s, SUB, MULT)
 
         def w2_codes(e, g, h):
             if (e, g) not in w2q:
@@ -134,11 +143,16 @@ def tile_moe_bdx_mlp_silu_kernel(tc, dyT, a, w2, w1, gate, offs, out):
             ws = codes.tile([P, HP * KH], U8, name="w1s", bufs=4, align_bytes=64)
             wb = stage.tile([P, PASS * J], BF16, name="wb", bufs=5, align_bytes=64)
             for h in range(HP):
-                lay(
-                    W1_ENGINE[(e * 2 + kh) * HP + h],
-                    wb[:, h * KH * J : (h + 1) * KH * J].rearrange("p (c i j) -> p c j i", i=4, j=J),
-                    w1raw[e, kh][:, h].rearrange("p j (c i) -> p c j i", i=4),
-                )
+                eng = W1_ENGINE[(e * 2 + kh) * HP + h]
+                part = wb[:, h * KH * J : (h + 1) * KH * J]
+                if eng == "G":
+                    lay(eng, part.rearrange("p (c j) -> p c j", j=J), w1raw[e, kh][:, h].rearrange("p j c -> p c j"))
+                else:
+                    lay(
+                        eng,
+                        part.rearrange("p (c i j) -> p c j i", i=4, j=J),
+                        w1raw[e, kh][:, h].rearrange("p j (c i) -> p c j i", i=4),
+                    )
             quant(wc[:], ws[:], wb[:])
             w1q[e, kh] = wc, ws
 
@@ -197,72 +211,72 @@ def tile_moe_bdx_mlp_silu_kernel(tc, dyT, a, w2, w1, gate, offs, out):
                 if e == E - 1:
                     nc.sync.dma_start(out[kt * P : (kt + 1) * P, :], outs[kt][:])
 
-        load_dy(0, 3)
         load_dy(0, 2)
-        load_dy(1, 2)
-        load_dy(1, 0)
-        gather(1, 0)
-        load_dy(1, 3)
-        load_a(0)
-        load_dy(1, 1)
-        load_dy(0, 0)
-        gather(1, 3)
+        load_dy(2, 1)
         load_dy(0, 1)
-        gather(1, 2)
-        gather(1, 1)
+        load_dy(0, 3)
+        load_dy(0, 0)
+        load_dy(1, 2)
+        gather(0, 1)
+        gather(0, 3)
         gather(0, 2)
         load_a(1)
-        gather(0, 3)
-        load_w2(0, 1)
-        g_codes(1)
-        load_dy(2, 3)
         load_dy(2, 0)
-        gather(0, 0)
         sigmoids(1)
-        gather(0, 1)
-        w2_codes(0, 1, 1)
-        load_dy(2, 2)
-        load_w2(0, 0)
-        load_dy(2, 1)
+        load_a(0)
         gather(2, 1)
         sigmoids(0)
-        silus(1)
-        load_w2(0, 2)
-        silus(0)
-        w2_codes(0, 0, 0)
-        w2_codes(0, 0, 1)
-        w2_codes(0, 2, 0)
-        load_w1(0, 0)
-        gather(2, 3)
-        w2_codes(0, 1, 0)
-        gather(2, 2)
-        g_codes(0)
+        load_dy(2, 2)
         gather(2, 0)
-        g_codes(2)
-        derivative(0)
+        load_dy(1, 3)
+        load_dy(2, 3)
+        load_w2(0, 1)
+        load_w2(0, 0)
+        gather(0, 0)
+        load_dy(1, 0)
+        load_dy(1, 1)
+        w2_codes(0, 1, 1)
+        w2_codes(0, 0, 0)
+        g_codes(0)
+        load_w2(0, 2)
+        w2_codes(0, 1, 0)
+        w2_codes(0, 0, 1)
+        gather(2, 2)
         load_w2(1, 0)
-        derivative(1)
+        w2_codes(1, 0, 0)
+        silus(1)
+        gather(2, 3)
+        silus(0)
+        gather(1, 0)
+        gather(1, 1)
+        gather(1, 2)
+        gather(1, 3)
+        g_codes(2)
+        load_w2(1, 1)
+        load_w1(0, 1)
+        w2_codes(0, 2, 0)
+        g_codes(1)
+        derivative(0)
         w2_codes(0, 2, 1)
         first_product(0, 0)
-        w1_codes(0, 0)
-        w2_codes(1, 0, 1)
-        load_w2(1, 1)
         first_product(0, 1)
-        w2_codes(1, 1, 1)
-        load_w2(1, 2)
-        load_w1(0, 1)
-        w2_codes(1, 0, 0)
-        load_w1(1, 0)
         w2_codes(1, 1, 0)
-        w2_codes(1, 2, 1)
+        load_w2(1, 2)
         load_w1(1, 1)
-        second_product(0, 0)
-        w1_codes(0, 1)
-        first_product(1, 1)
         w2_codes(1, 2, 0)
-        w1_codes(1, 0)
-        first_product(1, 0)
+        w1_codes(0, 1)
+        w2_codes(1, 0, 1)
+        w2_codes(1, 1, 1)
+        load_w1(0, 0)
+        w2_codes(1, 2, 1)
         w1_codes(1, 1)
+        w1_codes(0, 0)
+        derivative(1)
+        first_product(1, 0)
+        first_product(1, 1)
+        second_product(0, 0)
         second_product(0, 1)
+        load_w1(1, 0)
+        w1_codes(1, 0)
         second_product(1, 1)
         second_product(1, 0)

@@ -20,7 +20,7 @@ SIGMOID = mybir.ActivationFunctionType.Sigmoid
 SILU = mybir.ActivationFunctionType.Silu
 
 W2_ENGINE = "SSSSSSSSSSSS"
-W1_ENGINE = "SSSVSSVV"
+W1_ENGINE = "GSGSGSGS"
 G_ENGINE = "VVV"
 P = 128
 J = 4
@@ -62,7 +62,7 @@ def tile_moe_bdx_mlp_silu_kernel(tc, dyT, a, w2, w1, gate, offs, out):
         dy, gg, gq, w2raw, w2q, w1raw, w1q, dq = {}, {}, {}, {}, {}, {}, {}, {}
 
         def load_dy(g, j):
-            dy[g, j] = ring.tile([P, T], F32, name="dy", bufs=8)
+            dy[g, j] = ring.tile([P, T], F32, name="dy", bufs=12)
             nc.sync.dma_start(dy[g, j][:], dyT[g * PASS : (g + 1) * PASS, :].rearrange("(p j) t -> p j t", j=J)[:, j, :])
 
         act = held.tile([P, HP, J, SLOTS], F32, name="act")
@@ -98,7 +98,7 @@ def tile_moe_bdx_mlp_silu_kernel(tc, dyT, a, w2, w1, gate, offs, out):
             nc.vector.tensor_tensor(gg[g][:, j, :], dy[g, j][:].indirect(offsets[:]), gates[:], MULT)
 
         def g_codes(g):
-            gb = stage.tile([P, SLOTS * J], BF16, name="gb", bufs=2, align_bytes=64)
+            gb = stage.tile([P, SLOTS * J], BF16, name="gb", bufs=1, align_bytes=64)
             lay(
                 G_ENGINE[g],
                 gb[:].rearrange("p (c i j) -> p c j i", i=4, j=J),
@@ -130,7 +130,7 @@ def tile_moe_bdx_mlp_silu_kernel(tc, dyT, a, w2, w1, gate, offs, out):
                 w2q[e, g] = wc, ws
             wc, ws = w2q[e, g]
             cols = slice(h * PASS, (h + 1) * PASS)
-            wb = stage.tile([P, PASS * J], BF16, name="wb", bufs=5, align_bytes=64)
+            wb = stage.tile([P, PASS * J], BF16, name="wb", bufs=4, align_bytes=64)
             lay(
                 W2_ENGINE[(e * G + g) * HP + h],
                 wb[:].rearrange("p (t m j) -> p m j t", t=4, j=J),
@@ -139,9 +139,9 @@ def tile_moe_bdx_mlp_silu_kernel(tc, dyT, a, w2, w1, gate, offs, out):
             quant(wc[:, cols], ws[:, cols], wb[:])
 
         def w1_codes(e, kh):
-            wc = codes.tile([P, HP * KH], U32, name="w1c", bufs=4, align_bytes=64)
-            ws = codes.tile([P, HP * KH], U8, name="w1s", bufs=4, align_bytes=64)
-            wb = stage.tile([P, PASS * J], BF16, name="wb", bufs=5, align_bytes=64)
+            wc = codes.tile([P, HP * KH], U32, name="w1c", bufs=3, align_bytes=64)
+            ws = codes.tile([P, HP * KH], U8, name="w1s", bufs=3, align_bytes=64)
+            wb = stage.tile([P, PASS * J], BF16, name="w1b", bufs=2, align_bytes=64)
             for h in range(HP):
                 eng = W1_ENGINE[(e * 2 + kh) * HP + h]
                 part = wb[:, h * KH * J : (h + 1) * KH * J]
@@ -211,72 +211,72 @@ def tile_moe_bdx_mlp_silu_kernel(tc, dyT, a, w2, w1, gate, offs, out):
                 if e == E - 1:
                     nc.sync.dma_start(out[kt * P : (kt + 1) * P, :], outs[kt][:])
 
-        load_dy(0, 2)
-        load_dy(2, 1)
-        load_dy(0, 1)
-        load_dy(0, 3)
         load_dy(0, 0)
-        load_dy(1, 2)
-        gather(0, 1)
-        gather(0, 3)
-        gather(0, 2)
-        load_a(1)
-        load_dy(2, 0)
-        sigmoids(1)
+        load_dy(0, 1)
+        load_dy(0, 2)
+        load_dy(0, 3)
         load_a(0)
-        gather(2, 1)
-        sigmoids(0)
-        load_dy(2, 2)
-        gather(2, 0)
-        load_dy(1, 3)
-        load_dy(2, 3)
-        load_w2(0, 1)
-        load_w2(0, 0)
-        gather(0, 0)
         load_dy(1, 0)
         load_dy(1, 1)
-        w2_codes(0, 1, 1)
-        w2_codes(0, 0, 0)
-        g_codes(0)
+        load_dy(1, 2)
+        load_dy(1, 3)
+        load_a(1)
+        load_dy(2, 0)
+        load_dy(2, 1)
+        load_dy(2, 2)
+        load_dy(2, 3)
+        load_w2(0, 0)
+        load_w2(0, 1)
         load_w2(0, 2)
-        w2_codes(0, 1, 0)
-        w2_codes(0, 0, 1)
-        gather(2, 2)
-        load_w2(1, 0)
-        w2_codes(1, 0, 0)
-        silus(1)
-        gather(2, 3)
-        silus(0)
+        load_w1(0, 0)
+        load_w1(0, 1)
+        gather(0, 0)
+        gather(0, 1)
+        gather(0, 2)
+        gather(0, 3)
+        g_codes(0)
+        sigmoids(0)
         gather(1, 0)
         gather(1, 1)
         gather(1, 2)
         gather(1, 3)
-        g_codes(2)
-        load_w2(1, 1)
-        load_w1(0, 1)
-        w2_codes(0, 2, 0)
+        sigmoids(1)
         g_codes(1)
+        gather(2, 0)
+        gather(2, 1)
+        gather(2, 2)
+        gather(2, 3)
+        silus(0)
+        silus(1)
+        g_codes(2)
         derivative(0)
+        w2_codes(0, 0, 0)
+        w2_codes(0, 0, 1)
+        load_w2(1, 0)
+        w2_codes(0, 1, 0)
+        w2_codes(0, 1, 1)
+        load_w2(1, 1)
+        w2_codes(0, 2, 0)
         w2_codes(0, 2, 1)
+        load_w2(1, 2)
         first_product(0, 0)
         first_product(0, 1)
-        w2_codes(1, 1, 0)
-        load_w2(1, 2)
-        load_w1(1, 1)
-        w2_codes(1, 2, 0)
-        w1_codes(0, 1)
-        w2_codes(1, 0, 1)
-        w2_codes(1, 1, 1)
-        load_w1(0, 0)
-        w2_codes(1, 2, 1)
-        w1_codes(1, 1)
+        load_w1(1, 0)
         w1_codes(0, 0)
-        derivative(1)
-        first_product(1, 0)
-        first_product(1, 1)
+        w1_codes(0, 1)
         second_product(0, 0)
         second_product(0, 1)
-        load_w1(1, 0)
+        derivative(1)
+        load_w1(1, 1)
+        w2_codes(1, 0, 0)
+        w2_codes(1, 0, 1)
+        w2_codes(1, 1, 0)
+        w2_codes(1, 1, 1)
+        w2_codes(1, 2, 0)
+        w2_codes(1, 2, 1)
+        first_product(1, 0)
+        first_product(1, 1)
         w1_codes(1, 0)
-        second_product(1, 1)
         second_product(1, 0)
+        w1_codes(1, 1)
+        second_product(1, 1)

@@ -19,8 +19,8 @@ SUB = mybir.AluOpType.subtract
 SIGMOID = mybir.ActivationFunctionType.Sigmoid
 SILU = mybir.ActivationFunctionType.Silu
 
-W2_ENGINE = "SSSSSSSSSSSS"
-W1_ENGINE = "GSGSGSGS"
+W2_ENGINE = "SSSSVSVSSSSS"
+W1_ENGINE = "SSSSSSSS"
 G_ENGINE = "VVV"
 P = 128
 J = 4
@@ -79,7 +79,7 @@ def tile_moe_bdx_mlp_silu_kernel(tc, dyT, a, w2, w1, gate, offs, out):
             nc.sync.dma_start(w2raw[e, g][:], w2[e, g * PASS : (g + 1) * PASS, :].rearrange("(p j) i -> p j i", j=J))
 
         def load_w1(e, kh):
-            w1raw[e, kh] = ring.tile([P, HP, J, KH], F32, name="w1raw", bufs=3)
+            w1raw[e, kh] = ring.tile([P, HP, J, KH], F32, name="w1raw", bufs=2)
             rows = w1[e, :, kh * KH : (kh + 1) * KH].rearrange("(h p j) k -> p h j k", p=P, j=J)
             for h in range(HP):
                 nc.sync.dma_start(w1raw[e, kh][:, h], rows[:, h])
@@ -130,7 +130,7 @@ def tile_moe_bdx_mlp_silu_kernel(tc, dyT, a, w2, w1, gate, offs, out):
                 w2q[e, g] = wc, ws
             wc, ws = w2q[e, g]
             cols = slice(h * PASS, (h + 1) * PASS)
-            wb = stage.tile([P, PASS * J], BF16, name="wb", bufs=4, align_bytes=64)
+            wb = stage.tile([P, PASS * J], BF16, name="wb", bufs=5, align_bytes=64)
             lay(
                 W2_ENGINE[(e * G + g) * HP + h],
                 wb[:].rearrange("p (t m j) -> p m j t", t=4, j=J),
@@ -261,13 +261,13 @@ def tile_moe_bdx_mlp_silu_kernel(tc, dyT, a, w2, w1, gate, offs, out):
         load_w2(1, 2)
         first_product(0, 0)
         first_product(0, 1)
-        load_w1(1, 0)
         w1_codes(0, 0)
         w1_codes(0, 1)
+        load_w1(1, 0)
+        load_w1(1, 1)
         second_product(0, 0)
         second_product(0, 1)
         derivative(1)
-        load_w1(1, 1)
         w2_codes(1, 0, 0)
         w2_codes(1, 0, 1)
         w2_codes(1, 1, 0)

from contextlib import ExitStack

import concourse.mybir as mybir

N, T, H, K, E, C = 1536, 640, 1024, 512, 2, 256
SLOTS = E * C
FLOPS = 2 * SLOTS * (N * H + H * K)
BYTES = 4 * (N * T + H * SLOTS + E * N * H + E * H * K + SLOTS + K * T) + 2 * 128 * (SLOTS // 16)

F32 = mybir.dt.float32
BF16 = mybir.dt.bfloat16
U32 = mybir.dt.uint32
U16 = mybir.dt.uint16
U8 = mybir.dt.uint8
FP8X4 = mybir.dt.float8_e4m3fn_x4
MULT = mybir.AluOpType.mult
ADD = mybir.AluOpType.add
SUB = mybir.AluOpType.subtract
SIGMOID = mybir.ActivationFunctionType.Sigmoid
SILU = mybir.ActivationFunctionType.Silu

W2_ENGINE = "SSSSVSVSSSSS"
W1_ENGINE = "SSSSSSSS"
G_ENGINE = "VVV"
P = 128
J = 4
PASS = P * J
G = N // PASS
HP = H // PASS
KT = K // P
KH = K // 2


def tile_moe_bdx_mlp_silu_kernel(tc, dyT, a, w2, w1, gate, offs, out):
    nc = tc.nc
    with ExitStack() as ctx:
        held = ctx.enter_context(tc.tile_pool(name="held", bufs=1))
        codes = ctx.enter_context(tc.tile_pool(name="codes", bufs=4))
        ring = ctx.enter_context(tc.tile_pool(name="ring", bufs=3))
        stage = ctx.enter_context(tc.tile_pool(name="stage", bufs=2))
        psum = ctx.enter_context(tc.psum_pool(name="psum", bufs=4))

        offsets = held.tile([P, SLOTS // 16], U16, name="offsets")
        nc.sync.dma_start(offsets[:], offs)
        gates = held.tile([P, SLOTS], F32, name="gates")
        nc.sync.dma_start(gates[:], gate[0:P, :])

        one = held.tile([P, 1], F32, name="one")
        nc.vector.memset(one[:], 0.0)
        warm = held.tile([P, 1], F32, name="warm")
        nc.scalar.activation(warm[:], one[:], SIGMOID)

        outs = []
        for kt in range(KT):
            o = held.tile([P, T], F32, name=f"out{kt}")
            nc.gpsimd.memset(o[:], 0.0)
            outs.append(o)

        def quant(out_c, out_s, src):
            nc.vector.quantize_mx(out=out_c.bitcast(FP8X4), scales=out_s, in_=src)

        dy, gg, gq, w2raw, w2q, w1raw, w1q, dq = {}, {}, {}, {}, {}, {}, {}, {}

        def load_dy(g, j):
            dy[g, j] = ring.tile([P, T], F32, name="dy", bufs=12)
            nc.sync.dma_start(dy[g, j][:], dyT[g * PASS : (g + 1) * PASS, :].rearrange("(p j) t -> p j t", j=J)[:, j, :])

        act = held.tile([P, HP, J, SLOTS], F32, name="act")
        sig = held.tile([P, HP, J, SLOTS], F32, name="sig")
        PAIRS = [slice(0, 2), slice(2, 4)]

        def load_a(h):
            rows = a[h * PASS : (h + 1) * PASS, :].rearrange("(p t) n -> p t n", t=J)
            for pair in PAIRS:
                nc.sync.dma_start(act[:, h, pair, :], rows[:, pair, :])

        def load_w2(e, g):
            w2raw[e, g] = ring.tile([P, J, H], F32, name="w2raw", bufs=3)
            nc.sync.dma_start(w2raw[e, g][:], w2[e, g * PASS : (g + 1) * PASS, :].rearrange("(p j) i -> p j i", j=J))

        def load_w1(e, kh):
            w1raw[e, kh] = ring.tile([P, HP, J, KH], F32, name="w1raw", bufs=2)
            rows = w1[e, :, kh * KH : (kh + 1) * KH].rearrange("(h p j) k -> p h j k", p=P, j=J)
            for h in range(HP):
                nc.sync.dma_start(w1raw[e, kh][:, h], rows[:, h])

        def lay(engine, out_, in_):
            if engine == "V":
                nc.vector.tensor_copy(out_, in_)
            elif engine == "G":
                nc.gpsimd.tensor_scalar(out_, in_, 1.0, 0.0, MULT, ADD)
            else:
                nc.scalar.copy(out_, in_)

        def gather(g, j):
            if (g) not in gg:
                gg[g] = stage.tile([P, J, SLOTS], F32, name="gg", bufs=2)
            nc.vector.tensor_tensor(gg[g][:, j, :], dy[g, j][:].indirect(offsets[:]), gates[:], MULT)

        def g_codes(g):
            gb = stage.tile([P, SLOTS * J], BF16, name="gb", bufs=1, align_bytes=64)
            lay(
                G_ENGINE[g],
                gb[:].rearrange("p (c i j) -> p c j i", i=4, j=J),
                gg[g][:].rearrange("p j (c i) -> p c j i", i=4),
            )
            gc = held.tile([P, SLOTS], U32, name=f"gc{g}", align_bytes=64)
            gs = held.tile([P, SLOTS], U8, name=f"gs{g}", align_bytes=64)
            quant(gc[:], gs[:], gb[:])
            gq[g] = gc, gs

        def sigmoids(h):
            for pair in PAIRS:
                nc.scalar.activation(sig[:, h, pair, :], act[:, h, pair, :], SIGMOID)

        def silus(e):
            part = act[:, :, :, e * C : (e + 1) * C].rearrange("p h t n -> p (h t) n")
            nc.scalar.activation(part, part, SILU, scale=-1.0)

        def derivative(e):
            part = slice(e * C, (e + 1) * C)
            x = act[:, :, :, part].rearrange("p h t n -> p (h t) n")
            s = sig[:, :, :, part].rearrange("p h t n -> p (h t) n")
            nc.vector.scalar_tensor_tensor(s, x, 1.0, s, SUB, MULT)

        def w2_codes(e, g, h):
            if (e, g) not in w2q:
                wc = codes.tile([P, H], U32, name="w2c", bufs=4, align_bytes=64)
                ws = codes.tile([P, H], U8, name="w2s", bufs=4, align_bytes=64)
                w2q[e, g] = wc, ws
            wc, ws = w2q[e, g]
            cols = slice(h * PASS, (h + 1) * PASS)
            wb = stage.tile([P, PASS * J], BF16, name="wb", bufs=5, align_bytes=64)
            lay(
                W2_ENGINE[(e * G + g) * HP + h],
                wb[:].rearrange("p (t m j) -> p m j t", t=4, j=J),
                w2raw[e, g][:, :, cols].rearrange("p j (m t) -> p m j t", t=4),
            )
            quant(wc[:, cols], ws[:, cols], wb[:])

        def w1_codes(e, kh):
            wc = codes.tile([P, HP * KH], U32, name="w1c", bufs=3, align_bytes=64)
            ws = codes.tile([P, HP * KH], U8, name="w1s", bufs=3, align_bytes=64)
            wb = stage.tile([P, PASS * J], BF16, name="w1b", bufs=2, align_bytes=64)
            for h in range(HP):
                eng = W1_ENGINE[(e * 2 + kh) * HP + h]
                part = wb[:, h * KH * J : (h + 1) * KH * J]
                if eng == "G":
                    lay(eng, part.rearrange("p (c j) -> p c j", j=J), w1raw[e, kh][:, h].rearrange("p j c -> p c j"))
                else:
                    lay(
                        eng,
                        part.rearrange("p (c i j) -> p c j i", i=4, j=J),
                        w1raw[e, kh][:, h].rearrange("p j (c i) -> p c j i", i=4),
                    )
            quant(wc[:], ws[:], wb[:])
            w1q[e, kh] = wc, ws

        def first_product(e, h):
            db = stage.tile([P, C * J], BF16, name="db", bufs=2, align_bytes=64)
            for half in range(2):
                n0 = e * C + half * P
                bank = psum.tile([P, J, P], F32, name="dh", bufs=4)
                for t in range(J):
                    m = slice(h * PASS + t * P, h * PASS + (t + 1) * P)
                    for g in range(G):
                        wc, ws = w2q[e, g]
                        gc, gs = gq[g]
                        nc.tensor.matmul_mx(
                            out=bank[:, t, :],
                            lhsT=wc[:, m].bitcast(FP8X4),
                            lhsT_scale=ws[:, m],
                            rhs=gc[:, n0 : n0 + P].bitcast(FP8X4),
                            rhs_scale=gs[:, n0 : n0 + P],
                            start=(g == 0),
                            stop=(g == G - 1),
                        )
                nc.vector.scalar_tensor_tensor(
                    db[:, half * PASS : (half + 1) * PASS].rearrange("p (n t) -> p n t", t=J),
                    bank[:].rearrange("p t n -> p n t"),
                    -1.0,
                    sig[:, h, :, n0 : n0 + P].rearrange("p t n -> p n t"),
                    MULT,
                    MULT,
                )
            dc = codes.tile([P, C], U32, name="dc", bufs=4, align_bytes=64)
            ds = codes.tile([P, C], U8, name="ds", bufs=4, align_bytes=64)
            quant(dc[:], ds[:], db[:])
            dq[e, h] = dc, ds

        def second_product(e, kh):
            wc, ws = w1q[e, kh]
            for q in range(2):
                acc = psum.tile([P, C], F32, name="dx", bufs=4)
                for h in range(HP):
                    m = slice(h * KH + q * P, h * KH + (q + 1) * P)
                    dc, ds = dq[e, h]
                    nc.tensor.matmul_mx(
                        out=acc[:],
                        lhsT=wc[:, m].bitcast(FP8X4),
                        lhsT_scale=ws[:, m],
                        rhs=dc[:].bitcast(FP8X4),
                        rhs_scale=ds[:],
                        start=(h == 0),
                        stop=(h == HP - 1),
                    )
                dx = stage.tile([P, C], F32, name="dxs", bufs=4)
                nc.scalar.copy(out=dx[:], in_=acc[:])
                kt = 2 * kh + q
                nc.vector.tensor_copy(outs[kt][:].indirect(offsets[:, e * (C // 16) : (e + 1) * (C // 16)]), dx[:])
                if e == E - 1:
                    nc.sync.dma_start(out[kt * P : (kt + 1) * P, :], outs[kt][:])

        load_dy(0, 0)
        load_dy(0, 1)
        load_dy(0, 2)
        load_dy(0, 3)
        load_a(0)
        load_dy(1, 0)
        load_dy(1, 1)
        load_dy(1, 2)
        load_dy(1, 3)
        load_a(1)
        load_dy(2, 0)
        load_dy(2, 1)
        load_dy(2, 2)
        load_dy(2, 3)
        load_w2(0, 0)
        load_w2(0, 1)
        load_w2(0, 2)
        load_w1(0, 0)
        load_w1(0, 1)
        gather(0, 0)
        gather(0, 1)
        gather(0, 2)
        gather(0, 3)
        g_codes(0)
        sigmoids(0)
        gather(1, 0)
        gather(1, 1)
        gather(1, 2)
        gather(1, 3)
        sigmoids(1)
        g_codes(1)
        gather(2, 0)
        gather(2, 1)
        gather(2, 2)
        gather(2, 3)
        silus(0)
        silus(1)
        g_codes(2)
        derivative(0)
        w2_codes(0, 0, 0)
        w2_codes(0, 0, 1)
        load_w2(1, 0)
        w2_codes(0, 1, 0)
        w2_codes(0, 1, 1)
        load_w2(1, 1)
        w2_codes(0, 2, 0)
        w2_codes(0, 2, 1)
        load_w2(1, 2)
        first_product(0, 0)
        first_product(0, 1)
        w1_codes(0, 0)
        w1_codes(0, 1)
        load_w1(1, 0)
        load_w1(1, 1)
        second_product(0, 0)
        second_product(0, 1)
        derivative(1)
        w2_codes(1, 0, 0)
        w2_codes(1, 0, 1)
        w2_codes(1, 1, 0)
        w2_codes(1, 1, 1)
        w2_codes(1, 2, 0)
        w2_codes(1, 2, 1)
        first_product(1, 0)
        first_product(1, 1)
        w1_codes(1, 0)
        second_product(1, 0)
        w1_codes(1, 1)
        second_product(1, 1)
